import numpy as np
import ml_dtypes

BF16 = ml_dtypes.bfloat16


def bf(x):
    return np.asarray(x, np.float32).astype(BF16)


def f32(x):
    return np.asarray(x, np.float32)


def f64(x):
    return np.asarray(x).astype(np.float64)


def striped(idx):
    return np.tile(idx.reshape(-1, 16).T, (8, 1))


S, K, M, N = 512, 256, 512, 512


def setup_inputs():
    return {"base": bf(np.random.standard_normal((M, S))), "x": bf(np.random.standard_normal((K, N))), "w": bf(np.random.standard_normal((K, M)) / np.sqrt(K)), "s": f32(0.5 + np.random.random_sample((M, 1))), "b": f32(0.5 * np.random.standard_normal((M, 1))), "offs": striped(np.random.permutation(S))}


def reference(base, x, w, s, b, offs):
    idx = offs[:16].T.reshape(-1)
    z = f64(base).copy()
    z[:, idx] += f64(w).T @ f64(x)
    return z * f64(s) + f64(b)

@@ -1,0 +1,57 @@
+import concourse.mybir as mybir
+from concourse.masks import make_identity
+
+BF16, F32, U16 = mybir.dt.bfloat16, mybir.dt.float32, mybir.dt.uint16
+MULT, ADD = mybir.AluOpType.mult, mybir.AluOpType.add
+
+PARTS = 128
+FLOPS = 2 * 512 * 512 * 256
+
+
+def tile_scatter_matmul_kernel(tc, base, x, w, s, b, offs, out):
+    nc = tc.nc
+    m_rows, columns = base.shape
+    m_blocks = m_rows // PARTS
+    k_blocks = x.shape[0] // PARTS
+
+    with (
+        tc.tile_pool(name="held", bufs=1) as held,
+        tc.psum_pool(name="psum", bufs=1) as psum,
+    ):
+        base_t = held.tile([PARTS, m_blocks, columns], BF16)
+        x_t = held.tile([PARTS, k_blocks, x.shape[1]], BF16)
+        w_t = held.tile([PARTS, k_blocks, m_rows], BF16)
+        offsets = held.tile([PARTS, offs.shape[1]], U16)
+        s_t = held.tile([PARTS, m_blocks], F32)
+        b_t = held.tile([PARTS, m_blocks], F32)
+        ident = held.tile([PARTS, PARTS], BF16)
+        out_t = held.tile([PARTS, m_blocks, columns], F32)
+
+        nc.sync.dma_start(base_t[:], base.rearrange("(a p) t -> p a t", p=PARTS))
+        nc.sync.dma_start(offsets[:], offs)
+        nc.sync.dma_start(w_t[:], w.rearrange("(k p) m -> p k m", p=PARTS))
+        nc.sync.dma_start(x_t[:], x.rearrange("(k p) j -> p k j", p=PARTS))
+        nc.sync.dma_start(s_t[:], s.rearrange("(a p) o -> p (a o)", p=PARTS))
+        nc.sync.dma_start(b_t[:], b.rearrange("(a p) o -> p (a o)", p=PARTS))
+
+        make_identity(nc, ident[:])
+
+        windows = [psum.tile([PARTS, columns], F32, name=f"window{a}") for a in range(m_blocks)]
+        for a in range(m_blocks):
+            nc.tensor.matmul(windows[a][:], ident[:], base_t[:, a, :], start=True, stop=False)
+
+        for a in range(m_blocks):
+            for k in range(k_blocks):
+                nc.tensor.matmul(
+                    windows[a][:].indirect(offsets[:]),
+                    w_t[:, k, a * PARTS : (a + 1) * PARTS],
+                    x_t[:, k, :],
+                    start=False,
+                    stop=(k == k_blocks - 1),
+                )
+
+        for a in range(m_blocks):
+            nc.vector.tensor_scalar(
+                out_t[:, a, :], windows[a][:], s_t[:, a : a + 1], b_t[:, a : a + 1], op0=MULT, op1=ADD
+            )
+            nc.sync.dma_start(out[a * PARTS : (a + 1) * PARTS, :], out_t[:, a, :])

@@ -27,12 +27,12 @@ def tile_scatter_matmul_kernel(tc, base, x, w, s, b, offs, out):
         ident = held.tile([PARTS, PARTS], BF16)
         out_t = held.tile([PARTS, m_blocks, columns], F32)
 
-        nc.sync.dma_start(base_t[:], base.rearrange("(a p) t -> p a t", p=PARTS))
+        nc.sync.dma_start(base_t[:], base.rearrange("(p a) t -> p a t", p=PARTS))
         nc.sync.dma_start(offsets[:], offs)
-        nc.sync.dma_start(w_t[:], w.rearrange("(k p) m -> p k m", p=PARTS))
-        nc.sync.dma_start(x_t[:], x.rearrange("(k p) j -> p k j", p=PARTS))
-        nc.sync.dma_start(s_t[:], s.rearrange("(a p) o -> p (a o)", p=PARTS))
-        nc.sync.dma_start(b_t[:], b.rearrange("(a p) o -> p (a o)", p=PARTS))
+        nc.sync.dma_start(w_t[:], w.rearrange("(p k) m -> p k m", p=PARTS))
+        nc.sync.dma_start(x_t[:], x.rearrange("(p k) j -> p k j", p=PARTS))
+        nc.sync.dma_start(s_t[:], s.rearrange("(p a) o -> p (a o)", p=PARTS))
+        nc.sync.dma_start(b_t[:], b.rearrange("(p a) o -> p (a o)", p=PARTS))
 
         make_identity(nc, ident[:])
 
@@ -44,14 +44,15 @@ def tile_scatter_matmul_kernel(tc, base, x, w, s, b, offs, out):
             for k in range(k_blocks):
                 nc.tensor.matmul(
                     windows[a][:].indirect(offsets[:]),
-                    w_t[:, k, a * PARTS : (a + 1) * PARTS],
+                    w_t[:, k, a::m_blocks],
                     x_t[:, k, :],
                     start=False,
                     stop=(k == k_blocks - 1),
                 )
 
+        out_rows = out.rearrange("(p a) t -> p a t", p=PARTS)
         for a in range(m_blocks):
             nc.vector.tensor_scalar(
                 out_t[:, a, :], windows[a][:], s_t[:, a : a + 1], b_t[:, a : a + 1], op0=MULT, op1=ADD
             )
-            nc.sync.dma_start(out[a * PARTS : (a + 1) * PARTS, :], out_t[:, a, :])
+            nc.sync.dma_start(out_rows[:, a, :], out_t[:, a, :])

@@ -5,6 +5,7 @@ BF16, F32, U16 = mybir.dt.bfloat16, mybir.dt.float32, mybir.dt.uint16
 MULT, ADD = mybir.AluOpType.mult, mybir.AluOpType.add
 
 PARTS = 128
+WARM_UPS = 4
 FLOPS = 2 * 512 * 512 * 256
 
 
@@ -33,6 +34,12 @@ def tile_scatter_matmul_kernel(tc, base, x, w, s, b, offs, out):
         nc.sync.dma_start(x_t[:], x.rearrange("(p k) j -> p k j", p=PARTS))
         nc.sync.dma_start(s_t[:], s.rearrange("(p a) o -> p (a o)", p=PARTS))
         nc.sync.dma_start(b_t[:], b.rearrange("(p a) o -> p (a o)", p=PARTS))
+
+        zeros = held.tile([PARTS, columns], BF16)
+        nc.vector.memset(zeros[:], 0.0)
+        spare_bank = psum.tile([PARTS, columns], F32)
+        for i in range(WARM_UPS):
+            nc.tensor.matmul(spare_bank[:], zeros[:, :PARTS], zeros[:], start=True, stop=True)
 
         make_identity(nc, ident[:])
 

@@ -30,8 +30,11 @@ def tile_scatter_matmul_kernel(tc, base, x, w, s, b, offs, out):
 
         nc.sync.dma_start(base_t[:], base.rearrange("(p a) t -> p a t", p=PARTS))
         nc.sync.dma_start(offsets[:], offs)
-        nc.sync.dma_start(w_t[:], w.rearrange("(p k) m -> p k m", p=PARTS))
-        nc.sync.dma_start(x_t[:], x.rearrange("(p k) j -> p k j", p=PARTS))
+        w_rows = w.rearrange("(p k) m -> p k m", p=PARTS)
+        x_rows = x.rearrange("(p k) j -> p k j", p=PARTS)
+        for k in range(k_blocks):
+            nc.sync.dma_start(w_t[:, k, :], w_rows[:, k, :])
+            nc.sync.dma_start(x_t[:, k, :], x_rows[:, k, :])
         nc.sync.dma_start(s_t[:], s.rearrange("(p a) o -> p (a o)", p=PARTS))
         nc.sync.dma_start(b_t[:], b.rearrange("(p a) o -> p (a o)", p=PARTS))
 
@@ -47,8 +50,8 @@ def tile_scatter_matmul_kernel(tc, base, x, w, s, b, offs, out):
         for a in range(m_blocks):
             nc.tensor.matmul(windows[a][:], ident[:], base_t[:, a, :], start=True, stop=False)
 
-        for a in range(m_blocks):
-            for k in range(k_blocks):
+        for k in range(k_blocks):
+            for a in range(m_blocks):
                 nc.tensor.matmul(
                     windows[a][:].indirect(offsets[:]),
                     w_t[:, k, a::m_blocks],

import concourse.mybir as mybir
from concourse.masks import make_identity

BF16, F32, U16 = mybir.dt.bfloat16, mybir.dt.float32, mybir.dt.uint16
MULT, ADD = mybir.AluOpType.mult, mybir.AluOpType.add

PARTS = 128
WARM_UPS = 4
FLOPS = 2 * 512 * 512 * 256


def tile_scatter_matmul_kernel(tc, base, x, w, s, b, offs, out):
    nc = tc.nc
    m_rows, columns = base.shape
    m_blocks = m_rows // PARTS
    k_blocks = x.shape[0] // PARTS

    with (
        tc.tile_pool(name="held", bufs=1) as held,
        tc.psum_pool(name="psum", bufs=1) as psum,
    ):
        base_t = held.tile([PARTS, m_blocks, columns], BF16)
        x_t = held.tile([PARTS, k_blocks, x.shape[1]], BF16)
        w_t = held.tile([PARTS, k_blocks, m_rows], BF16)
        offsets = held.tile([PARTS, offs.shape[1]], U16)
        s_t = held.tile([PARTS, m_blocks], F32)
        b_t = held.tile([PARTS, m_blocks], F32)
        ident = held.tile([PARTS, PARTS], BF16)
        out_t = held.tile([PARTS, m_blocks, columns], F32)

        nc.sync.dma_start(base_t[:], base.rearrange("(p a) t -> p a t", p=PARTS))
        nc.sync.dma_start(offsets[:], offs)
        w_rows = w.rearrange("(p k) m -> p k m", p=PARTS)
        x_rows = x.rearrange("(p k) j -> p k j", p=PARTS)
        for k in range(k_blocks):
            nc.sync.dma_start(w_t[:, k, :], w_rows[:, k, :])
            nc.sync.dma_start(x_t[:, k, :], x_rows[:, k, :])
        nc.sync.dma_start(s_t[:], s.rearrange("(p a) o -> p (a o)", p=PARTS))
        nc.sync.dma_start(b_t[:], b.rearrange("(p a) o -> p (a o)", p=PARTS))

        zeros = held.tile([PARTS, columns], BF16)
        nc.vector.memset(zeros[:], 0.0)
        spare_bank = psum.tile([PARTS, columns], F32)
        for i in range(WARM_UPS):
            nc.tensor.matmul(spare_bank[:], zeros[:, :PARTS], zeros[:], start=True, stop=True)

        make_identity(nc, ident[:])

        windows = [psum.tile([PARTS, columns], F32, name=f"window{a}") for a in range(m_blocks)]
        for a in range(m_blocks):
            nc.tensor.matmul(windows[a][:], ident[:], base_t[:, a, :], start=True, stop=False)

        for k in range(k_blocks):
            for a in range(m_blocks):
                nc.tensor.matmul(
                    windows[a][:].indirect(offsets[:]),
                    w_t[:, k, a::m_blocks],
                    x_t[:, k, :],
                    start=False,
                    stop=(k == k_blocks - 1),
                )

        out_rows = out.rearrange("(p a) t -> p a t", p=PARTS)
        for a in range(m_blocks):
            nc.vector.tensor_scalar(
                out_t[:, a, :], windows[a][:], s_t[:, a : a + 1], b_t[:, a : a + 1], op0=MULT, op1=ADD
            )
            nc.sync.dma_start(out_rows[:, a, :], out_t[:, a, :])
